import numpy as np
import ml_dtypes


def mxq(x, axis, fmt="e4m3"):
    dtype, down = {"e4m3": (ml_dtypes.float8_e4m3fn, 7), "e5m2": (ml_dtypes.float8_e5m2, 14)}[fmt]
    v = np.moveaxis(np.asarray(x, np.float32).astype(ml_dtypes.bfloat16).astype(np.float64), axis, -1)
    blocks = v.reshape(v.shape[:-1] + (-1, 32))
    amax = np.abs(blocks).max(-1, keepdims=True)
    byte = np.maximum(np.where(amax > 0, np.frexp(amax)[1] - 1 + 127, 0) - down, 1)
    scale = np.exp2(byte - 127.0)
    codes = (blocks / scale).astype(np.float32).astype(dtype).astype(np.float64)
    return np.moveaxis((codes * scale).reshape(v.shape), -1, axis)


WIDE = False


def mx_kscale(k):
    if not WIDE:
        return np.ones(k)
    levels = np.array([10, -10, 5, -5, 0])
    if k % 512:
        return np.exp2(np.random.permutation(np.resize(levels, k // 32))).repeat(32)
    a = np.empty((k // 512, 16))
    for p in range(k // 512):
        a[p, :8] = np.random.permutation(np.resize(levels, 8))
        for g in range(8):
            far = levels[np.abs(levels - a[p, g]) >= 10]
            a[p, g + 8] = far[np.random.randint(len(far))]
    return np.exp2(a.ravel()).repeat(32)


def f64(x):
    return np.asarray(x).astype(np.float64)


def striped(idx):
    return np.tile(np.asarray(idx).reshape(-1, 16).T, (8, 1)).astype(np.uint16)


def unstriped(offs):
    return offs[:16].T.reshape(-1).astype(np.int64)


E2M1 = np.array([0.0, 0.5, 1.0, 1.5, 2.0, 3.0, 4.0, 6.0, -0.0, -0.5, -1.0, -1.5, -2.0, -3.0, -4.0, -6.0])


def pack_weight(w, fmt):
    k, n = w.shape
    w = f64(np.asarray(w, np.float32).astype(ml_dtypes.bfloat16)).reshape(k // 32, 32, n)
    amax = np.abs(w).max(1)
    if fmt == "e4m3":
        byte = np.frexp(amax)[1] - 1 + 127 - 7
    else:
        mant, ex = np.frexp(amax / 6.0)
        byte = np.where(mant > 0.5, ex, ex - 1) + 127
    byte = np.clip(np.where(amax > 0, byte, 1), 1, 254)
    scaled = (w * np.exp2(127.0 - byte)[:, None, :]).reshape(k, n).astype(np.float32)
    by_word = np.ascontiguousarray(scaled.reshape(k // 512, 128, 4, n).transpose(0, 1, 3, 2))
    if fmt == "e4m3":
        words = by_word.astype(ml_dtypes.float8_e4m3fn).view(np.uint8)
    else:
        c = by_word.astype(ml_dtypes.float4_e2m1fn).view(np.uint8) & 0xF
        words = (c[..., 0::2] | (c[..., 1::2] << 4)).reshape(k // 512, 128, 2 * n)
    return np.ascontiguousarray(words), np.ascontiguousarray(byte.astype(np.uint8).reshape(k // 512, 16, n))


def unpack_weight(words, scales, fmt):
    g, _, n = scales.shape
    words = np.ascontiguousarray(words).reshape(g, 128, n, -1)
    if fmt == "e4m3":
        vals = words.view(ml_dtypes.float8_e4m3fn).astype(np.float64)
    else:
        nib = np.empty((g, 128, n, 4), np.uint8)
        nib[..., 0::2] = words & 0xF
        nib[..., 1::2] = words >> 4
        vals = E2M1[nib]
    vals = vals * np.repeat(np.exp2(scales.astype(np.float64) - 127.0), 8, axis=1)[..., None]
    return vals.transpose(0, 1, 3, 2).reshape(g * 512, n)


D, T, I, J, U, Z, E = 512, 2048, 512, 512, 1024, 1024, 512


def setup_inputs():
    n = np.random.standard_normal
    idx = np.random.permutation(T)[:I]
    idx2 = np.random.permutation(U)[:J]
    idx3 = np.random.permutation(Z)[:J]
    fd = mx_kscale(D)
    fi = mx_kscale(I)
    ti = np.ones(T)
    ti[idx] = fi
    keysp = pack_weight(n((D, T)) / fd[:, None], "e4m3")
    return {
        "keys_words": keysp[0],
        "keys_scales": keysp[1],
        "notes": (n((D, U)) * 1.0 / np.sqrt(D) * fd[:, None]).astype(np.float32),
        "users2": (n((D, Z)) * 1.0 / np.sqrt(D) * fd[:, None]).astype(np.float32),
        "rowf": (np.random.uniform(0.02, 0.08, (I, 1)) * fi[:, None]).astype(np.float32),
        "vals": (n((E, T)) / ti).astype(np.float32),
        "offs": striped(idx),
        "offs2": striped(idx2),
        "offs3": striped(idx3),
    }


def reference(keys_words, keys_scales, notes, users2, rowf, vals, offs, offs2, offs3):
    idx = unstriped(offs)
    idx2 = unstriped(offs2)
    idx3 = unstriped(offs3)
    keysu = unpack_weight(keys_words, keys_scales, "e4m3")
    keysidxg = keysu[:, idx]
    notesq = mxq(f64(notes), 0, "e4m3")
    g1 = keysidxg.T @ notesq
    users2idx3q = mxq(f64(users2)[:, idx3], 0, "e4m3")
    g2 = keysidxg.T @ users2idx3q
    g0 = np.maximum(g1[:, idx2], g2)
    gr1 = g0 * f64(rowf)
    vt1 = f64(vals)[:, idx].T
    vt1q = mxq(vt1, 0, "e4m3")
    gr1q = mxq(gr1, 0, "e4m3")
    o = vt1q.T @ gr1q
    return o

@@ -1,0 +1,201 @@
+from contextlib import ExitStack
+
+import concourse.mybir as mybir
+from concourse.masks import make_identity
+
+D, T, I, J, U, Z, E = 512, 2048, 512, 512, 1024, 1024, 512
+FLOPS = 2 * D * I * U + 2 * D * I * J + 2 * I * E * J
+
+F32 = mybir.dt.float32
+BF16 = mybir.dt.bfloat16
+U32 = mybir.dt.uint32
+I32 = mybir.dt.int32
+U16 = mybir.dt.uint16
+U8 = mybir.dt.uint8
+FP8X4 = mybir.dt.float8_e4m3fn_x4
+COPY = mybir.ActivationFunctionType.Copy
+MULT = mybir.AluOpType.mult
+MAX = mybir.AluOpType.max
+
+P = 128
+PACK = 4
+BANK = 512
+RUN = 4
+
+
+def woven(dst, src):
+    return (
+        dst.rearrange("p (c i) t -> p c t i", i=RUN),
+        src.rearrange("p t (c i) -> p c t i", i=RUN),
+    )
+
+
+def tile_attend_tab_wideandown_exchange_kernel(
+    tc, keys_words, keys_scales, notes, users2, rowf, vals, offs, offs2, offs3, out
+):
+    nc = tc.nc
+    with ExitStack() as ctx:
+        sb = ctx.enter_context(tc.tile_pool(name="sb", bufs=1))
+        ps = ctx.enter_context(tc.psum_pool(name="ps", bufs=1))
+
+        def tile(shape, dtype, name):
+            return sb.tile(shape, dtype, name=name, align_bytes=64)
+
+        def bank(b, shape, name):
+            return ps.tile(shape, F32, name=name, tag="bank%d" % b)
+
+        def quantise(src, width, name):
+            codes = tile([P, width], U32, name + "_codes")
+            scales = tile([P, width], U8, name + "_scales")
+            nc.vector.quantize_mx(out=codes[:].bitcast(FP8X4), scales=scales[:], in_=src)
+            return codes, scales
+
+        key_list = tile([P, I // 16], U16, "key_list")
+        note_list = tile([P, J // 16], U16, "note_list")
+        user_list = tile([P, J // 16], U16, "user_list")
+        pool_words = tile([P, T], U32, "pool_words")
+        pool_bytes = tile([P, T], U8, "pool_bytes")
+        notes_raw = [tile([P, PACK, BANK], F32, "notes_raw%d" % h) for h in range(2)]
+        users_raw = [tile([P, Z], F32, "users_raw%d" % t) for t in range(PACK)]
+        vals_raw = [tile([P, T], F32, "vals_raw%d" % b) for b in range(E // P)]
+        row_factor = tile([P, PACK], F32, "row_factor")
+
+        landed_bytes = tile([P, T], U8, "landed_bytes")
+        nc.vector.memset(pool_bytes[:].bitcast(I32), 0)
+        for q in range(4):
+            nc.scalar.dma_start(
+                out=landed_bytes[32 * q : 32 * q + 4, :].bitcast(I32),
+                in_=keys_scales[0, 4 * q : 4 * q + 4, :].bitcast(I32),
+            )
+        notes_planes = notes.rearrange("(p t) u -> p t u", t=PACK)
+        users_planes = users2.rearrange("(p t) z -> p t z", t=PACK)
+        nc.sync.dma_start(key_list[:], offs)
+        nc.sync.dma_start(out=notes_raw[0][:], in_=notes_planes[:, :, 0:BANK])
+        nc.sync.dma_start(
+            out=pool_words[:].bitcast(I32),
+            in_=keys_words[0].rearrange("p n t -> p (n t)").bitcast(I32),
+        )
+        nc.sync.dma_start(out=notes_raw[1][:], in_=notes_planes[:, :, BANK:U])
+        nc.sync.dma_start(user_list[:], offs3)
+        nc.sync.dma_start(note_list[:], offs2)
+        for t in range(PACK):
+            nc.sync.dma_start(out=users_raw[t][:], in_=users_planes[:, t, :])
+        nc.sync.dma_start(out=row_factor[:], in_=rowf.rearrange("(p t) o -> p (t o)", t=PACK))
+        for b in range(E // P):
+            nc.sync.dma_start(out=vals_raw[b][:], in_=vals[P * b : P * (b + 1), :])
+
+        ident = tile([P, P], F32, "ident")
+        make_identity(nc, ident[:])
+
+        for q in range(4):
+            rows = slice(32 * q, 32 * q + 4)
+            nc.vector.tensor_copy(pool_bytes[rows, :].bitcast(I32), landed_bytes[rows, :].bitcast(I32))
+        key_words = tile([P, PACK, P], U32, "key_words")
+        key_bytes = tile([P, PACK, P], U8, "key_bytes")
+        nc.vector.tensor_copy(
+            key_bytes[:].rearrange("p t s -> p s t"), pool_bytes[:].indirect(key_list[:])
+        )
+
+        notes_bf = [tile([P, BANK, PACK], BF16, "notes_bf%d" % h) for h in range(2)]
+        split = 384
+        nc.vector.tensor_copy(*woven(notes_bf[0][:, 0:split, :], notes_raw[0][:, :, 0:split]))
+        dst, src = woven(notes_bf[0][:, split:BANK, :], notes_raw[0][:, :, split:BANK])
+        nc.scalar.activation(dst, src, COPY)
+        notes_q = [quantise(notes_bf[0][:].rearrange("p u t -> p (u t)"), BANK, "notes0")]
+        nc.vector.tensor_copy(
+            key_words[:].rearrange("p t s -> p s t"), pool_words[:].indirect(key_list[:])
+        )
+
+        def keys_times(dst, t, moving):
+            nc.tensor.matmul_mx(
+                out=dst,
+                lhsT=key_words[:, t, :].bitcast(FP8X4),
+                lhsT_scale=key_bytes[:, t, :],
+                rhs=moving[0][:].bitcast(FP8X4),
+                rhs_scale=moving[1][:],
+                start=True,
+                stop=True,
+            )
+
+        wide = [tile([P, U], F32, "wide%d" % t) for t in range(PACK)]
+        for t in range(PACK):
+            acc = bank(t, [P, BANK], "wide_acc0_%d" % t)
+            keys_times(acc[:], t, notes_q[0])
+            nc.scalar.copy(wide[t][:, 0:BANK], acc[:])
+
+        nc.vector.tensor_copy(*woven(notes_bf[1][:], notes_raw[1][:]))
+        notes_q.append(quantise(notes_bf[1][:].rearrange("p u t -> p (u t)"), BANK, "notes1"))
+
+        picked = [tile([P, J], F32, "picked%d" % t) for t in range(PACK)]
+        wide_acc = [bank(PACK + t, [P, BANK], "wide_acc1_%d" % t) for t in range(PACK)]
+        for t in range(PACK):
+            keys_times(wide_acc[t][:], t, notes_q[1])
+        for pair in range(2):
+            for t in (2 * pair, 2 * pair + 1):
+                nc.scalar.copy(wide[t][:, BANK:U], wide_acc[t][:])
+            for t in (2 * pair, 2 * pair + 1):
+                nc.scalar.activation(picked[t][:], wide[t][:].indirect(note_list[:]), COPY)
+
+        users_got = tile([P, PACK, J], BF16, "users_got")
+        for t in range(PACK):
+            nc.vector.tensor_copy(users_got[:, t, :], users_raw[t][:].indirect(user_list[:]))
+        users_bf = tile([P, J, PACK], BF16, "users_bf")
+        nc.vector.tensor_copy(*woven(users_bf[:], users_got[:]))
+        users_q = quantise(users_bf[:].rearrange("p j t -> p (j t)"), J, "users")
+
+        vals_got = [tile([P, I], BF16, "vals_got%d" % b) for b in range(E // P)]
+        vals_bf = [tile([P, P, 2], F32, "vals_bf%d" % b) for b in range(E // P)]
+
+        def turn_values(b):
+            words = vals_got[b][:].bitcast(F32)
+            turned = bank(PACK + b, [P, 2, P], "turned%d" % b)
+            for u in range(2):
+                nc.tensor.transpose(turned[:, u, :], words[:, u : I // 2 : 2], ident[:])
+            nc.scalar.copy(vals_bf[b][:], turned[:].rearrange("p u e -> p e u"))
+
+        nc.vector.tensor_copy(vals_got[0][:], vals_raw[0][:].indirect(key_list[:]))
+
+        larger = [tile([P, J], F32, "larger%d" % t) for t in range(PACK)]
+        table_planes = tile([P, PACK, J], BF16, "table_planes")
+        for t in range(PACK):
+            narrow = bank(t, [P, J], "narrow%d" % t)
+            keys_times(narrow[:], t, users_q)
+            nc.vector.tensor_tensor(larger[t][:], narrow[:], picked[t][:], MAX)
+        for t in range(PACK):
+            nc.vector.tensor_scalar(
+                table_planes[:, t, :], larger[t][:], row_factor[:, t : t + 1], None, MULT
+            )
+        turn_values(0)
+        for b in range(1, E // P):
+            nc.scalar.activation(vals_got[b][:], vals_raw[b][:].indirect(key_list[:]), COPY)
+            turn_values(b)
+
+        table_bf = tile([P, J, PACK], BF16, "table_bf")
+        nc.vector.tensor_copy(*woven(table_bf[:], table_planes[:]))
+        vals_q = [
+            quantise(vals_bf[b][:].rearrange("p e u -> p (e u)").bitcast(BF16), P, "vals%d" % b)
+            for b in range(2)
+        ]
+        table_q = quantise(table_bf[:].rearrange("p j t -> p (j t)"), J, "table")
+        for b in range(2, E // P):
+            vals_q.append(
+                quantise(vals_bf[b][:].rearrange("p e u -> p (e u)").bitcast(BF16), P, "vals%d" % b)
+            )
+
+        for b in range(E // P):
+            acc = bank(b, [P, J], "out_acc%d" % b)
+            nc.tensor.matmul_mx(
+                out=acc[:],
+                lhsT=vals_q[b][0][:].bitcast(FP8X4),
+                lhsT_scale=vals_q[b][1][:],
+                rhs=table_q[0][:].bitcast(FP8X4),
+                rhs_scale=table_q[1][:],
+                start=True,
+                stop=True,
+            )
+            result = tile([P, J], F32, "result%d" % b)
+            if b % 2 == 0:
+                nc.scalar.copy(result[:], acc[:])
+            else:
+                nc.vector.tensor_copy(result[:], acc[:])
+            nc.sync.dma_start(out=out[P * b : P * (b + 1), :], in_=result[:])

@@ -15,12 +15,16 @@ U8 = mybir.dt.uint8
 FP8X4 = mybir.dt.float8_e4m3fn_x4
 COPY = mybir.ActivationFunctionType.Copy
 MULT = mybir.AluOpType.mult
+ADD = mybir.AluOpType.add
 MAX = mybir.AluOpType.max
 
 P = 128
 PACK = 4
 BANK = 512
 RUN = 4
+SLOT = 4096
+HALF = 256
+AT_NOTES, AT_WIDE, AT_VALS2, AT_VALS3 = 0, SLOT, 2 * SLOT, 4 * SLOT
 
 
 def woven(dst, src):
@@ -38,14 +42,18 @@ def tile_attend_tab_wideandown_exchange_kernel(
         sb = ctx.enter_context(tc.tile_pool(name="sb", bufs=1))
         ps = ctx.enter_context(tc.psum_pool(name="ps", bufs=1))
 
-        def tile(shape, dtype, name):
-            return sb.tile(shape, dtype, name=name, align_bytes=64)
+        reuse = ctx.enter_context(tc.tile_pool(name="reuse", bufs=1))
+
+        def tile(shape, dtype, name, at=None):
+            if at is None:
+                return sb.tile(shape, dtype, name=name, align_bytes=64)
+            return reuse.tile(shape, dtype, name=name, align_bytes=64, offset=at)
 
         def bank(b, shape, name):
             return ps.tile(shape, F32, name=name, tag="bank%d" % b)
 
-        def quantise(src, width, name):
-            codes = tile([P, width], U32, name + "_codes")
+        def quantise(src, width, name, at=None):
+            codes = tile([P, width], U32, name + "_codes", at)
             scales = tile([P, width], U8, name + "_scales")
             nc.vector.quantize_mx(out=codes[:].bitcast(FP8X4), scales=scales[:], in_=src)
             return codes, scales
@@ -57,20 +65,20 @@ def tile_attend_tab_wideandown_exchange_kernel(
         pool_bytes = tile([P, T], U8, "pool_bytes")
         notes_raw = [tile([P, PACK, BANK], F32, "notes_raw%d" % h) for h in range(2)]
         users_raw = [tile([P, Z], F32, "users_raw%d" % t) for t in range(PACK)]
-        vals_raw = [tile([P, T], F32, "vals_raw%d" % b) for b in range(E // P)]
+        raw_at = [None, None, AT_VALS2, AT_VALS3]
+        vals_raw = [tile([P, T], F32, "vals_raw%d" % b, raw_at[b]) for b in range(E // P)]
         row_factor = tile([P, PACK], F32, "row_factor")
 
-        landed_bytes = tile([P, T], U8, "landed_bytes")
-        nc.vector.memset(pool_bytes[:].bitcast(I32), 0)
-        for q in range(4):
-            nc.scalar.dma_start(
-                out=landed_bytes[32 * q : 32 * q + 4, :].bitcast(I32),
-                in_=keys_scales[0, 4 * q : 4 * q + 4, :].bitcast(I32),
-            )
+        nc.gpsimd.memset(pool_bytes[:].bitcast(I32), 0)
         notes_planes = notes.rearrange("(p t) u -> p t u", t=PACK)
         users_planes = users2.rearrange("(p t) z -> p t z", t=PACK)
-        nc.sync.dma_start(key_list[:], offs)
         nc.sync.dma_start(out=notes_raw[0][:], in_=notes_planes[:, :, 0:BANK])
+        for q in range(4):
+            nc.sync.dma_start(
+                out=pool_bytes[32 * q : 32 * q + 4, :].bitcast(I32),
+                in_=keys_scales[0, 4 * q : 4 * q + 4, :].bitcast(I32),
+            )
+        nc.sync.dma_start(key_list[:], offs)
         nc.sync.dma_start(
             out=pool_words[:].bitcast(I32),
             in_=keys_words[0].rearrange("p n t -> p (n t)").bitcast(I32),
@@ -87,37 +95,54 @@ def tile_attend_tab_wideandown_exchange_kernel(
         ident = tile([P, P], F32, "ident")
         make_identity(nc, ident[:])
 
-        for q in range(4):
-            rows = slice(32 * q, 32 * q + 4)
-            nc.vector.tensor_copy(pool_bytes[rows, :].bitcast(I32), landed_bytes[rows, :].bitcast(I32))
         key_words = tile([P, PACK, P], U32, "key_words")
         key_bytes = tile([P, PACK, P], U8, "key_bytes")
-        nc.vector.tensor_copy(
-            key_bytes[:].rearrange("p t s -> p s t"), pool_bytes[:].indirect(key_list[:])
-        )
 
-        notes_bf = [tile([P, BANK, PACK], BF16, "notes_bf%d" % h) for h in range(2)]
-        split = 384
+        notes_bf = [
+            tile([P, BANK, PACK], BF16, "notes_bf0"),
+            tile([P, BANK, PACK], BF16, "notes_bf1", AT_NOTES),
+        ]
+        split = 128
         nc.vector.tensor_copy(*woven(notes_bf[0][:, 0:split, :], notes_raw[0][:, :, 0:split]))
         dst, src = woven(notes_bf[0][:, split:BANK, :], notes_raw[0][:, :, split:BANK])
         nc.scalar.activation(dst, src, COPY)
         notes_q = [quantise(notes_bf[0][:].rearrange("p u t -> p (u t)"), BANK, "notes0")]
         nc.vector.tensor_copy(
+            key_bytes[:].rearrange("p t s -> p s t"), pool_bytes[:].indirect(key_list[:])
+        )
+        nc.vector.tensor_copy(
             key_words[:].rearrange("p t s -> p s t"), pool_words[:].indirect(key_list[:])
         )
 
-        def keys_times(dst, t, moving):
+        def weave_and_quantise(planes, name):
+            side_by_side = tile([P, J, PACK], BF16, name + "_bf")
+            codes = tile([P, J], U32, name + "_codes")
+            scales = tile([P, J], U8, name + "_scales")
+            halves = [slice(0, HALF), slice(HALF, J)]
+            for cols in halves:
+                nc.vector.tensor_copy(*woven(side_by_side[:, cols, :], planes[:, :, cols]))
+            for cols in halves:
+                nc.vector.quantize_mx(
+                    out=codes[:, cols].bitcast(FP8X4),
+                    scales=scales[:, cols],
+                    in_=side_by_side[:, cols, :].rearrange("p j t -> p (j t)"),
+                )
+            return codes, scales
+
+        def keys_times(dst, t, moving, cols=slice(0, BANK)):
             nc.tensor.matmul_mx(
                 out=dst,
                 lhsT=key_words[:, t, :].bitcast(FP8X4),
                 lhsT_scale=key_bytes[:, t, :],
-                rhs=moving[0][:].bitcast(FP8X4),
-                rhs_scale=moving[1][:],
+                rhs=moving[0][:, cols].bitcast(FP8X4),
+                rhs_scale=moving[1][:, cols],
                 start=True,
                 stop=True,
             )
 
-        wide = [tile([P, U], F32, "wide%d" % t) for t in range(PACK)]
+        wide = [
+            tile([P, U], F32, "wide%d" % t, AT_WIDE if t == PACK - 1 else None) for t in range(PACK)
+        ]
         for t in range(PACK):
             acc = bank(t, [P, BANK], "wide_acc0_%d" % t)
             keys_times(acc[:], t, notes_q[0])
@@ -136,65 +161,74 @@ def tile_attend_tab_wideandown_exchange_kernel(
             for t in (2 * pair, 2 * pair + 1):
                 nc.scalar.activation(picked[t][:], wide[t][:].indirect(note_list[:]), COPY)
 
-        users_got = tile([P, PACK, J], BF16, "users_got")
+        users_got = tile([P, PACK, J], BF16, "users_got", AT_NOTES)
         for t in range(PACK):
             nc.vector.tensor_copy(users_got[:, t, :], users_raw[t][:].indirect(user_list[:]))
-        users_bf = tile([P, J, PACK], BF16, "users_bf")
-        nc.vector.tensor_copy(*woven(users_bf[:], users_got[:]))
-        users_q = quantise(users_bf[:].rearrange("p j t -> p (j t)"), J, "users")
-
-        vals_got = [tile([P, I], BF16, "vals_got%d" % b) for b in range(E // P)]
-        vals_bf = [tile([P, P, 2], F32, "vals_bf%d" % b) for b in range(E // P)]
-
-        def turn_values(b):
-            words = vals_got[b][:].bitcast(F32)
-            turned = bank(PACK + b, [P, 2, P], "turned%d" % b)
-            for u in range(2):
-                nc.tensor.transpose(turned[:, u, :], words[:, u : I // 2 : 2], ident[:])
-            nc.scalar.copy(vals_bf[b][:], turned[:].rearrange("p u e -> p e u"))
-
-        nc.vector.tensor_copy(vals_got[0][:], vals_raw[0][:].indirect(key_list[:]))
+        users_q = weave_and_quantise(users_got, "users")
 
         larger = [tile([P, J], F32, "larger%d" % t) for t in range(PACK)]
         table_planes = tile([P, PACK, J], BF16, "table_planes")
         for t in range(PACK):
             narrow = bank(t, [P, J], "narrow%d" % t)
-            keys_times(narrow[:], t, users_q)
+            for cols in (slice(0, HALF), slice(HALF, J)):
+                keys_times(narrow[:, cols], t, users_q, cols)
             nc.vector.tensor_tensor(larger[t][:], narrow[:], picked[t][:], MAX)
-        for t in range(PACK):
-            nc.vector.tensor_scalar(
-                table_planes[:, t, :], larger[t][:], row_factor[:, t : t + 1], None, MULT
+            engine = nc.vector if t == PACK - 1 else nc.gpsimd
+            engine.tensor_scalar(
+                table_planes[:, t, :], larger[t][:], row_factor[:, t : t + 1], 0.0, MULT, ADD
             )
-        turn_values(0)
-        for b in range(1, E // P):
-            nc.scalar.activation(vals_got[b][:], vals_raw[b][:].indirect(key_list[:]), COPY)
-            turn_values(b)
 
-        table_bf = tile([P, J, PACK], BF16, "table_bf")
-        nc.vector.tensor_copy(*woven(table_bf[:], table_planes[:]))
-        vals_q = [
-            quantise(vals_bf[b][:].rearrange("p e u -> p (e u)").bitcast(BF16), P, "vals%d" % b)
-            for b in range(2)
-        ]
-        table_q = quantise(table_bf[:].rearrange("p j t -> p (j t)"), J, "table")
-        for b in range(2, E // P):
-            vals_q.append(
-                quantise(vals_bf[b][:].rearrange("p e u -> p (e u)").bitcast(BF16), P, "vals%d" % b)
+        vals_got = [tile([P, I], BF16, "vals_got%d" % b, AT_WIDE + 1024 * b) for b in range(E // P)]
+        first_two = tile([P, 2, P, 2], F32, "first_two", AT_VALS2)
+        last_two = [tile([P, P, 2], F32, "vals_bf%d" % b) for b in (2, 3)]
+
+        def gather_values(b):
+            nc.scalar.activation(vals_got[b][:], vals_raw[b][:].indirect(key_list[:]), COPY)
+
+        def turn_values(b, turned):
+            words = vals_got[b][:].bitcast(F32)
+            for u in range(2):
+                nc.tensor.transpose(turned[:, u, :], words[:, u : I // 2 : 2], ident[:])
+
+        for b in range(3):
+            gather_values(b)
+        turned01 = bank(1, [P, 2, 2, P], "turned01")
+        for b in range(2):
+            turn_values(b, turned01[:, b])
+        nc.scalar.copy(first_two[:], turned01[:].rearrange("p b u e -> p b e u"))
+        gather_values(3)
+        for b in (2, 3):
+            turned = bank(2 * (b - 2), [P, 2, P], "turned%d" % b)
+            turn_values(b, turned)
+            nc.scalar.copy(last_two[b - 2][:], turned[:].rearrange("p u e -> p e u"))
+
+        table_q = weave_and_quantise(table_planes, "table")
+        codes, scales = quantise(
+            first_two[:].rearrange("p b e u -> p (b e u)").bitcast(BF16), 2 * P, "vals01", AT_VALS3
+        )
+        vals_q = [(codes[:, P * b : P * (b + 1)], scales[:, P * b : P * (b + 1)]) for b in range(2)]
+        for b in (2, 3):
+            codes, scales = quantise(
+                last_two[b - 2][:].rearrange("p e u -> p (e u)").bitcast(BF16),
+                P,
+                "vals%d" % b,
+                AT_VALS3 + 512 * b,
             )
+            vals_q.append((codes[:], scales[:]))
 
         for b in range(E // P):
-            acc = bank(b, [P, J], "out_acc%d" % b)
+            acc = bank(PACK + b, [P, J], "out_acc%d" % b)
             nc.tensor.matmul_mx(
                 out=acc[:],
-                lhsT=vals_q[b][0][:].bitcast(FP8X4),
-                lhsT_scale=vals_q[b][1][:],
+                lhsT=vals_q[b][0].bitcast(FP8X4),
+                lhsT_scale=vals_q[b][1],
                 rhs=table_q[0][:].bitcast(FP8X4),
                 rhs_scale=table_q[1][:],
                 start=True,
                 stop=True,
             )
             result = tile([P, J], F32, "result%d" % b)
-            if b % 2 == 0:
+            if b in (1, 2):
                 nc.scalar.copy(result[:], acc[:])
             else:
                 nc.vector.tensor_copy(result[:], acc[:])

@@ -24,7 +24,9 @@ BANK = 512
 RUN = 4
 SLOT = 4096
 HALF = 256
-AT_NOTES, AT_WIDE, AT_VALS2, AT_VALS3 = 0, SLOT, 2 * SLOT, 4 * SLOT
+AT_NOTES, AT_USERS, AT_WIDE = 0, SLOT, 2 * SLOT
+AT_VALS0, AT_VALS2, AT_VALS3 = 3 * SLOT, 5 * SLOT, 7 * SLOT
+HALVES = (slice(0, HALF), slice(HALF, BANK))
 
 
 def woven(dst, src):
@@ -65,7 +67,7 @@ def tile_attend_tab_wideandown_exchange_kernel(
         pool_bytes = tile([P, T], U8, "pool_bytes")
         notes_raw = [tile([P, PACK, BANK], F32, "notes_raw%d" % h) for h in range(2)]
         users_raw = [tile([P, Z], F32, "users_raw%d" % t) for t in range(PACK)]
-        raw_at = [None, None, AT_VALS2, AT_VALS3]
+        raw_at = [AT_VALS0, None, AT_VALS2, AT_VALS3]
         vals_raw = [tile([P, T], F32, "vals_raw%d" % b, raw_at[b]) for b in range(E // P)]
         row_factor = tile([P, PACK], F32, "row_factor")
 
@@ -73,10 +75,10 @@ def tile_attend_tab_wideandown_exchange_kernel(
         notes_planes = notes.rearrange("(p t) u -> p t u", t=PACK)
         users_planes = users2.rearrange("(p t) z -> p t z", t=PACK)
         nc.sync.dma_start(out=notes_raw[0][:], in_=notes_planes[:, :, 0:BANK])
-        for q in range(4):
+        for r in range(4):
             nc.sync.dma_start(
-                out=pool_bytes[32 * q : 32 * q + 4, :].bitcast(I32),
-                in_=keys_scales[0, 4 * q : 4 * q + 4, :].bitcast(I32),
+                out=pool_bytes[r:P:32, :].bitcast(I32),
+                in_=keys_scales[0, r:16:4, :].bitcast(I32),
             )
         nc.sync.dma_start(key_list[:], offs)
         nc.sync.dma_start(
@@ -98,10 +100,7 @@ def tile_attend_tab_wideandown_exchange_kernel(
         key_words = tile([P, PACK, P], U32, "key_words")
         key_bytes = tile([P, PACK, P], U8, "key_bytes")
 
-        notes_bf = [
-            tile([P, BANK, PACK], BF16, "notes_bf0"),
-            tile([P, BANK, PACK], BF16, "notes_bf1", AT_NOTES),
-        ]
+        notes_bf = [tile([P, BANK, PACK], BF16, "notes_bf0")]
         split = 128
         nc.vector.tensor_copy(*woven(notes_bf[0][:, 0:split, :], notes_raw[0][:, :, 0:split]))
         dst, src = woven(notes_bf[0][:, split:BANK, :], notes_raw[0][:, :, split:BANK])
@@ -114,28 +113,27 @@ def tile_attend_tab_wideandown_exchange_kernel(
             key_words[:].rearrange("p t s -> p s t"), pool_words[:].indirect(key_list[:])
         )
 
-        def weave_and_quantise(planes, name):
-            side_by_side = tile([P, J, PACK], BF16, name + "_bf")
-            codes = tile([P, J], U32, name + "_codes")
-            scales = tile([P, J], U8, name + "_scales")
-            halves = [slice(0, HALF), slice(HALF, J)]
-            for cols in halves:
+        def weave_and_quantise(planes, name, woven_at=None, codes_at=None):
+            side_by_side = tile([P, BANK, PACK], BF16, name + "_bf", woven_at)
+            for cols in HALVES:
                 nc.vector.tensor_copy(*woven(side_by_side[:, cols, :], planes[:, :, cols]))
-            for cols in halves:
-                nc.vector.quantize_mx(
-                    out=codes[:, cols].bitcast(FP8X4),
-                    scales=scales[:, cols],
-                    in_=side_by_side[:, cols, :].rearrange("p j t -> p (j t)"),
+            return [
+                quantise(
+                    side_by_side[:, cols, :].rearrange("p j t -> p (j t)"),
+                    HALF,
+                    "%s%d" % (name, h),
+                    None if codes_at is None else codes_at + 4 * HALF * h,
                 )
-            return codes, scales
+                for h, cols in enumerate(HALVES)
+            ]
 
-        def keys_times(dst, t, moving, cols=slice(0, BANK)):
+        def keys_times(dst, t, moving):
             nc.tensor.matmul_mx(
                 out=dst,
                 lhsT=key_words[:, t, :].bitcast(FP8X4),
                 lhsT_scale=key_bytes[:, t, :],
-                rhs=moving[0][:, cols].bitcast(FP8X4),
-                rhs_scale=moving[1][:, cols],
+                rhs=moving[0][:].bitcast(FP8X4),
+                rhs_scale=moving[1][:],
                 start=True,
                 stop=True,
             )
@@ -148,13 +146,13 @@ def tile_attend_tab_wideandown_exchange_kernel(
             keys_times(acc[:], t, notes_q[0])
             nc.scalar.copy(wide[t][:, 0:BANK], acc[:])
 
-        nc.vector.tensor_copy(*woven(notes_bf[1][:], notes_raw[1][:]))
-        notes_q.append(quantise(notes_bf[1][:].rearrange("p u t -> p (u t)"), BANK, "notes1"))
+        notes1_q = weave_and_quantise(notes_raw[1], "notes1", AT_NOTES)
 
         picked = [tile([P, J], F32, "picked%d" % t) for t in range(PACK)]
         wide_acc = [bank(PACK + t, [P, BANK], "wide_acc1_%d" % t) for t in range(PACK)]
         for t in range(PACK):
-            keys_times(wide_acc[t][:], t, notes_q[1])
+            for h, cols in enumerate(HALVES):
+                keys_times(wide_acc[t][:, cols], t, notes1_q[h])
         for pair in range(2):
             for t in (2 * pair, 2 * pair + 1):
                 nc.scalar.copy(wide[t][:, BANK:U], wide_acc[t][:])
@@ -164,21 +162,24 @@ def tile_attend_tab_wideandown_exchange_kernel(
         users_got = tile([P, PACK, J], BF16, "users_got", AT_NOTES)
         for t in range(PACK):
             nc.vector.tensor_copy(users_got[:, t, :], users_raw[t][:].indirect(user_list[:]))
-        users_q = weave_and_quantise(users_got, "users")
+        users_q = weave_and_quantise(users_got, "users", AT_USERS)
 
-        larger = [tile([P, J], F32, "larger%d" % t) for t in range(PACK)]
+        got_at = [AT_USERS] + [AT_WIDE + 1024 * b for b in range(1, E // P)]
+        vals_got = [tile([P, I], BF16, "vals_got%d" % b, got_at[b]) for b in range(E // P)]
+        nc.vector.tensor_copy(vals_got[0][:], vals_raw[0][:].indirect(key_list[:]))
+
+        larger = [tile([P, J], F32, "larger%d" % t, AT_VALS0 + 4 * J * t) for t in range(PACK)]
         table_planes = tile([P, PACK, J], BF16, "table_planes")
         for t in range(PACK):
             narrow = bank(t, [P, J], "narrow%d" % t)
-            for cols in (slice(0, HALF), slice(HALF, J)):
-                keys_times(narrow[:, cols], t, users_q, cols)
+            for h, cols in enumerate(HALVES):
+                keys_times(narrow[:, cols], t, users_q[h])
             nc.vector.tensor_tensor(larger[t][:], narrow[:], picked[t][:], MAX)
             engine = nc.vector if t == PACK - 1 else nc.gpsimd
             engine.tensor_scalar(
                 table_planes[:, t, :], larger[t][:], row_factor[:, t : t + 1], 0.0, MULT, ADD
             )
 
-        vals_got = [tile([P, I], BF16, "vals_got%d" % b, AT_WIDE + 1024 * b) for b in range(E // P)]
         first_two = tile([P, 2, P, 2], F32, "first_two", AT_VALS2)
         last_two = [tile([P, P, 2], F32, "vals_bf%d" % b) for b in (2, 3)]
 
@@ -190,21 +191,21 @@ def tile_attend_tab_wideandown_exchange_kernel(
             for u in range(2):
                 nc.tensor.transpose(turned[:, u, :], words[:, u : I // 2 : 2], ident[:])
 
-        for b in range(3):
+        for b in (1, 2):
             gather_values(b)
-        turned01 = bank(1, [P, 2, 2, P], "turned01")
+        turned01 = bank(0, [P, 2, 2, P], "turned01")
         for b in range(2):
             turn_values(b, turned01[:, b])
         nc.scalar.copy(first_two[:], turned01[:].rearrange("p b u e -> p b e u"))
         gather_values(3)
         for b in (2, 3):
-            turned = bank(2 * (b - 2), [P, 2, P], "turned%d" % b)
+            turned = bank(b - 1, [P, 2, P], "turned%d" % b)
             turn_values(b, turned)
             nc.scalar.copy(last_two[b - 2][:], turned[:].rearrange("p u e -> p e u"))
 
-        table_q = weave_and_quantise(table_planes, "table")
+        table_q = weave_and_quantise(table_planes, "table", None, AT_VALS3)
         codes, scales = quantise(
-            first_two[:].rearrange("p b e u -> p (b e u)").bitcast(BF16), 2 * P, "vals01", AT_VALS3
+            first_two[:].rearrange("p b e u -> p (b e u)").bitcast(BF16), 2 * P, "vals01"
         )
         vals_q = [(codes[:, P * b : P * (b + 1)], scales[:, P * b : P * (b + 1)]) for b in range(2)]
         for b in (2, 3):
@@ -212,24 +213,32 @@ def tile_attend_tab_wideandown_exchange_kernel(
                 last_two[b - 2][:].rearrange("p e u -> p (e u)").bitcast(BF16),
                 P,
                 "vals%d" % b,
-                AT_VALS3 + 512 * b,
             )
             vals_q.append((codes[:], scales[:]))
 
-        for b in range(E // P):
-            acc = bank(PACK + b, [P, J], "out_acc%d" % b)
+        out_acc = [bank(PACK + b, [P, J], "out_acc%d" % b) for b in range(E // P)]
+
+        def values_times_table(b, h):
             nc.tensor.matmul_mx(
-                out=acc[:],
+                out=out_acc[b][:, HALVES[h]],
                 lhsT=vals_q[b][0].bitcast(FP8X4),
                 lhsT_scale=vals_q[b][1],
-                rhs=table_q[0][:].bitcast(FP8X4),
-                rhs_scale=table_q[1][:],
+                rhs=table_q[h][0][:].bitcast(FP8X4),
+                rhs_scale=table_q[h][1][:],
                 start=True,
                 stop=True,
             )
+
+        for h in range(2):
+            for b in range(2):
+                values_times_table(b, h)
+        for b in (2, 3):
+            for h in range(2):
+                values_times_table(b, h)
+        for b in range(E // P):
             result = tile([P, J], F32, "result%d" % b)
-            if b in (1, 2):
-                nc.scalar.copy(result[:], acc[:])
+            if b % 2 == 0:
+                nc.scalar.copy(result[:], out_acc[b][:])
             else:
-                nc.vector.tensor_copy(result[:], acc[:])
+                nc.vector.tensor_copy(result[:], out_acc[b][:])
             nc.sync.dma_start(out=out[P * b : P * (b + 1), :], in_=result[:])

@@ -24,8 +24,7 @@ BANK = 512
 RUN = 4
 SLOT = 4096
 HALF = 256
-AT_NOTES, AT_USERS, AT_WIDE = 0, SLOT, 2 * SLOT
-AT_VALS0, AT_VALS2, AT_VALS3 = 3 * SLOT, 5 * SLOT, 7 * SLOT
+AT_NOTES, AT_WIDE, AT_VALS3 = 0, SLOT, 2 * SLOT
 HALVES = (slice(0, HALF), slice(HALF, BANK))
 
 
@@ -67,7 +66,7 @@ def tile_attend_tab_wideandown_exchange_kernel(
         pool_bytes = tile([P, T], U8, "pool_bytes")
         notes_raw = [tile([P, PACK, BANK], F32, "notes_raw%d" % h) for h in range(2)]
         users_raw = [tile([P, Z], F32, "users_raw%d" % t) for t in range(PACK)]
-        raw_at = [AT_VALS0, None, AT_VALS2, AT_VALS3]
+        raw_at = [None, None, None, AT_VALS3]
         vals_raw = [tile([P, T], F32, "vals_raw%d" % b, raw_at[b]) for b in range(E // P)]
         row_factor = tile([P, PACK], F32, "row_factor")
 
@@ -75,10 +74,10 @@ def tile_attend_tab_wideandown_exchange_kernel(
         notes_planes = notes.rearrange("(p t) u -> p t u", t=PACK)
         users_planes = users2.rearrange("(p t) z -> p t z", t=PACK)
         nc.sync.dma_start(out=notes_raw[0][:], in_=notes_planes[:, :, 0:BANK])
-        for r in range(4):
+        for q in range(4):
             nc.sync.dma_start(
-                out=pool_bytes[r:P:32, :].bitcast(I32),
-                in_=keys_scales[0, r:16:4, :].bitcast(I32),
+                out=pool_bytes[32 * q : 32 * q + 4, :].bitcast(I32),
+                in_=keys_scales[0, 4 * q : 4 * q + 4, :].bitcast(I32),
             )
         nc.sync.dma_start(key_list[:], offs)
         nc.sync.dma_start(
@@ -162,83 +161,59 @@ def tile_attend_tab_wideandown_exchange_kernel(
         users_got = tile([P, PACK, J], BF16, "users_got", AT_NOTES)
         for t in range(PACK):
             nc.vector.tensor_copy(users_got[:, t, :], users_raw[t][:].indirect(user_list[:]))
-        users_q = weave_and_quantise(users_got, "users", AT_USERS)
+        users_q = weave_and_quantise(users_got, "users")
 
-        got_at = [AT_USERS] + [AT_WIDE + 1024 * b for b in range(1, E // P)]
-        vals_got = [tile([P, I], BF16, "vals_got%d" % b, got_at[b]) for b in range(E // P)]
-        nc.vector.tensor_copy(vals_got[0][:], vals_raw[0][:].indirect(key_list[:]))
-
-        larger = [tile([P, J], F32, "larger%d" % t, AT_VALS0 + 4 * J * t) for t in range(PACK)]
+        larger = [tile([P, J], F32, "larger%d" % t) for t in range(PACK)]
         table_planes = tile([P, PACK, J], BF16, "table_planes")
         for t in range(PACK):
             narrow = bank(t, [P, J], "narrow%d" % t)
             for h, cols in enumerate(HALVES):
                 keys_times(narrow[:, cols], t, users_q[h])
-            nc.vector.tensor_tensor(larger[t][:], narrow[:], picked[t][:], MAX)
+            nc.vector.tensor_tensor(larger[t][:], picked[t][:], narrow[:], MAX)
             engine = nc.vector if t == PACK - 1 else nc.gpsimd
             engine.tensor_scalar(
                 table_planes[:, t, :], larger[t][:], row_factor[:, t : t + 1], 0.0, MULT, ADD
             )
 
-        first_two = tile([P, 2, P, 2], F32, "first_two", AT_VALS2)
-        last_two = [tile([P, P, 2], F32, "vals_bf%d" % b) for b in (2, 3)]
-
-        def gather_values(b):
-            nc.scalar.activation(vals_got[b][:], vals_raw[b][:].indirect(key_list[:]), COPY)
-
-        def turn_values(b, turned):
-            words = vals_got[b][:].bitcast(F32)
-            for u in range(2):
-                nc.tensor.transpose(turned[:, u, :], words[:, u : I // 2 : 2], ident[:])
-
-        for b in (1, 2):
-            gather_values(b)
-        turned01 = bank(0, [P, 2, 2, P], "turned01")
-        for b in range(2):
-            turn_values(b, turned01[:, b])
-        nc.scalar.copy(first_two[:], turned01[:].rearrange("p b u e -> p b e u"))
-        gather_values(3)
-        for b in (2, 3):
-            turned = bank(b - 1, [P, 2, P], "turned%d" % b)
-            turn_values(b, turned)
-            nc.scalar.copy(last_two[b - 2][:], turned[:].rearrange("p u e -> p e u"))
-
-        table_q = weave_and_quantise(table_planes, "table", None, AT_VALS3)
-        codes, scales = quantise(
-            first_two[:].rearrange("p b e u -> p (b e u)").bitcast(BF16), 2 * P, "vals01"
-        )
-        vals_q = [(codes[:, P * b : P * (b + 1)], scales[:, P * b : P * (b + 1)]) for b in range(2)]
-        for b in (2, 3):
-            codes, scales = quantise(
-                last_two[b - 2][:].rearrange("p e u -> p (e u)").bitcast(BF16),
-                P,
-                "vals%d" % b,
-            )
-            vals_q.append((codes[:], scales[:]))
-
-        out_acc = [bank(PACK + b, [P, J], "out_acc%d" % b) for b in range(E // P)]
-
-        def values_times_table(b, h):
-            nc.tensor.matmul_mx(
-                out=out_acc[b][:, HALVES[h]],
-                lhsT=vals_q[b][0].bitcast(FP8X4),
-                lhsT_scale=vals_q[b][1],
-                rhs=table_q[h][0][:].bitcast(FP8X4),
-                rhs_scale=table_q[h][1][:],
-                start=True,
-                stop=True,
-            )
-
-        for h in range(2):
-            for b in range(2):
-                values_times_table(b, h)
-        for b in (2, 3):
-            for h in range(2):
-                values_times_table(b, h)
+        vals_got = [tile([P, I], BF16, "vals_got%d" % b, AT_WIDE + 1024 * b) for b in range(E // P)]
         for b in range(E // P):
+            nc.scalar.activation(vals_got[b][:], vals_raw[b][:].indirect(key_list[:]), COPY)
+        vals_bf = []
+        for pair in range(2):
+            turned = bank(pair, [P, 2, 2, P], "turned%d" % pair)
+            for b in range(2):
+                words = vals_got[2 * pair + b][:].bitcast(F32)
+                for u in range(2):
+                    nc.tensor.transpose(turned[:, b, u, :], words[:, u : I // 2 : 2], ident[:])
+            vals_bf.append(tile([P, 2, P, 2], F32, "vals_bf%d" % pair, AT_VALS3 + 2048 * pair))
+            nc.scalar.copy(vals_bf[pair][:], turned[:].rearrange("p b u e -> p b e u"))
+
+        table_q = weave_and_quantise(table_planes, "table")
+        vals_q = []
+        for pair in range(2):
+            codes, scales = quantise(
+                vals_bf[pair][:].rearrange("p b e u -> p (b e u)").bitcast(BF16),
+                2 * P,
+                "vals%d" % pair,
+            )
+            for b in range(2):
+                vals_q.append((codes[:, P * b : P * (b + 1)], scales[:, P * b : P * (b + 1)]))
+
+        for b in range(E // P):
+            acc = bank(PACK + b, [P, J], "out_acc%d" % b)
+            for h, cols in enumerate(HALVES):
+                nc.tensor.matmul_mx(
+                    out=acc[:, cols],
+                    lhsT=vals_q[b][0].bitcast(FP8X4),
+                    lhsT_scale=vals_q[b][1],
+                    rhs=table_q[h][0][:].bitcast(FP8X4),
+                    rhs_scale=table_q[h][1][:],
+                    start=True,
+                    stop=True,
+                )
             result = tile([P, J], F32, "result%d" % b)
             if b % 2 == 0:
-                nc.scalar.copy(result[:], out_acc[b][:])
+                nc.scalar.copy(result[:], acc[:])
             else:
-                nc.vector.tensor_copy(result[:], out_acc[b][:])
+                nc.vector.tensor_copy(result[:], acc[:])
             nc.sync.dma_start(out=out[P * b : P * (b + 1), :], in_=result[:])

from contextlib import ExitStack

import concourse.mybir as mybir
from concourse.masks import make_identity

D, T, I, J, U, Z, E = 512, 2048, 512, 512, 1024, 1024, 512
FLOPS = 2 * D * I * U + 2 * D * I * J + 2 * I * E * J

F32 = mybir.dt.float32
BF16 = mybir.dt.bfloat16
U32 = mybir.dt.uint32
I32 = mybir.dt.int32
U16 = mybir.dt.uint16
U8 = mybir.dt.uint8
FP8X4 = mybir.dt.float8_e4m3fn_x4
COPY = mybir.ActivationFunctionType.Copy
MULT = mybir.AluOpType.mult
ADD = mybir.AluOpType.add
MAX = mybir.AluOpType.max

P = 128
PACK = 4
BANK = 512
RUN = 4
SLOT = 4096
HALF = 256
AT_NOTES, AT_WIDE, AT_VALS3 = 0, SLOT, 2 * SLOT
HALVES = (slice(0, HALF), slice(HALF, BANK))


def woven(dst, src):
    return (
        dst.rearrange("p (c i) t -> p c t i", i=RUN),
        src.rearrange("p t (c i) -> p c t i", i=RUN),
    )


def tile_attend_tab_wideandown_exchange_kernel(
    tc, keys_words, keys_scales, notes, users2, rowf, vals, offs, offs2, offs3, out
):
    nc = tc.nc
    with ExitStack() as ctx:
        sb = ctx.enter_context(tc.tile_pool(name="sb", bufs=1))
        ps = ctx.enter_context(tc.psum_pool(name="ps", bufs=1))

        reuse = ctx.enter_context(tc.tile_pool(name="reuse", bufs=1))

        def tile(shape, dtype, name, at=None):
            if at is None:
                return sb.tile(shape, dtype, name=name, align_bytes=64)
            return reuse.tile(shape, dtype, name=name, align_bytes=64, offset=at)

        def bank(b, shape, name):
            return ps.tile(shape, F32, name=name, tag="bank%d" % b)

        def quantise(src, width, name, at=None):
            codes = tile([P, width], U32, name + "_codes", at)
            scales = tile([P, width], U8, name + "_scales")
            nc.vector.quantize_mx(out=codes[:].bitcast(FP8X4), scales=scales[:], in_=src)
            return codes, scales

        key_list = tile([P, I // 16], U16, "key_list")
        note_list = tile([P, J // 16], U16, "note_list")
        user_list = tile([P, J // 16], U16, "user_list")
        pool_words = tile([P, T], U32, "pool_words")
        pool_bytes = tile([P, T], U8, "pool_bytes")
        notes_raw = [tile([P, PACK, BANK], F32, "notes_raw%d" % h) for h in range(2)]
        users_raw = [tile([P, Z], F32, "users_raw%d" % t) for t in range(PACK)]
        raw_at = [None, None, None, AT_VALS3]
        vals_raw = [tile([P, T], F32, "vals_raw%d" % b, raw_at[b]) for b in range(E // P)]
        row_factor = tile([P, PACK], F32, "row_factor")

        nc.gpsimd.memset(pool_bytes[:].bitcast(I32), 0)
        notes_planes = notes.rearrange("(p t) u -> p t u", t=PACK)
        users_planes = users2.rearrange("(p t) z -> p t z", t=PACK)
        nc.sync.dma_start(out=notes_raw[0][:], in_=notes_planes[:, :, 0:BANK])
        for q in range(4):
            nc.sync.dma_start(
                out=pool_bytes[32 * q : 32 * q + 4, :].bitcast(I32),
                in_=keys_scales[0, 4 * q : 4 * q + 4, :].bitcast(I32),
            )
        nc.sync.dma_start(key_list[:], offs)
        nc.sync.dma_start(
            out=pool_words[:].bitcast(I32),
            in_=keys_words[0].rearrange("p n t -> p (n t)").bitcast(I32),
        )
        nc.sync.dma_start(out=notes_raw[1][:], in_=notes_planes[:, :, BANK:U])
        nc.sync.dma_start(user_list[:], offs3)
        nc.sync.dma_start(note_list[:], offs2)
        for t in range(PACK):
            nc.sync.dma_start(out=users_raw[t][:], in_=users_planes[:, t, :])
        nc.sync.dma_start(out=row_factor[:], in_=rowf.rearrange("(p t) o -> p (t o)", t=PACK))
        for b in range(E // P):
            nc.sync.dma_start(out=vals_raw[b][:], in_=vals[P * b : P * (b + 1), :])

        ident = tile([P, P], F32, "ident")
        make_identity(nc, ident[:])

        key_words = tile([P, PACK, P], U32, "key_words")
        key_bytes = tile([P, PACK, P], U8, "key_bytes")

        notes_bf = [tile([P, BANK, PACK], BF16, "notes_bf0")]
        split = 128
        nc.vector.tensor_copy(*woven(notes_bf[0][:, 0:split, :], notes_raw[0][:, :, 0:split]))
        dst, src = woven(notes_bf[0][:, split:BANK, :], notes_raw[0][:, :, split:BANK])
        nc.scalar.activation(dst, src, COPY)
        notes_q = [quantise(notes_bf[0][:].rearrange("p u t -> p (u t)"), BANK, "notes0")]
        nc.vector.tensor_copy(
            key_bytes[:].rearrange("p t s -> p s t"), pool_bytes[:].indirect(key_list[:])
        )
        nc.vector.tensor_copy(
            key_words[:].rearrange("p t s -> p s t"), pool_words[:].indirect(key_list[:])
        )

        def weave_and_quantise(planes, name, woven_at=None, codes_at=None):
            side_by_side = tile([P, BANK, PACK], BF16, name + "_bf", woven_at)
            for cols in HALVES:
                nc.vector.tensor_copy(*woven(side_by_side[:, cols, :], planes[:, :, cols]))
            return [
                quantise(
                    side_by_side[:, cols, :].rearrange("p j t -> p (j t)"),
                    HALF,
                    "%s%d" % (name, h),
                    None if codes_at is None else codes_at + 4 * HALF * h,
                )
                for h, cols in enumerate(HALVES)
            ]

        def keys_times(dst, t, moving):
            nc.tensor.matmul_mx(
                out=dst,
                lhsT=key_words[:, t, :].bitcast(FP8X4),
                lhsT_scale=key_bytes[:, t, :],
                rhs=moving[0][:].bitcast(FP8X4),
                rhs_scale=moving[1][:],
                start=True,
                stop=True,
            )

        wide = [
            tile([P, U], F32, "wide%d" % t, AT_WIDE if t == PACK - 1 else None) for t in range(PACK)
        ]
        for t in range(PACK):
            acc = bank(t, [P, BANK], "wide_acc0_%d" % t)
            keys_times(acc[:], t, notes_q[0])
            nc.scalar.copy(wide[t][:, 0:BANK], acc[:])

        notes1_q = weave_and_quantise(notes_raw[1], "notes1", AT_NOTES)

        picked = [tile([P, J], F32, "picked%d" % t) for t in range(PACK)]
        wide_acc = [bank(PACK + t, [P, BANK], "wide_acc1_%d" % t) for t in range(PACK)]
        for t in range(PACK):
            for h, cols in enumerate(HALVES):
                keys_times(wide_acc[t][:, cols], t, notes1_q[h])
        for pair in range(2):
            for t in (2 * pair, 2 * pair + 1):
                nc.scalar.copy(wide[t][:, BANK:U], wide_acc[t][:])
            for t in (2 * pair, 2 * pair + 1):
                nc.scalar.activation(picked[t][:], wide[t][:].indirect(note_list[:]), COPY)

        users_got = tile([P, PACK, J], BF16, "users_got", AT_NOTES)
        for t in range(PACK):
            nc.vector.tensor_copy(users_got[:, t, :], users_raw[t][:].indirect(user_list[:]))
        users_q = weave_and_quantise(users_got, "users")

        larger = [tile([P, J], F32, "larger%d" % t) for t in range(PACK)]
        table_planes = tile([P, PACK, J], BF16, "table_planes")
        for t in range(PACK):
            narrow = bank(t, [P, J], "narrow%d" % t)
            for h, cols in enumerate(HALVES):
                keys_times(narrow[:, cols], t, users_q[h])
            nc.vector.tensor_tensor(larger[t][:], picked[t][:], narrow[:], MAX)
            engine = nc.vector if t == PACK - 1 else nc.gpsimd
            engine.tensor_scalar(
                table_planes[:, t, :], larger[t][:], row_factor[:, t : t + 1], 0.0, MULT, ADD
            )

        vals_got = [tile([P, I], BF16, "vals_got%d" % b, AT_WIDE + 1024 * b) for b in range(E // P)]
        for b in range(E // P):
            nc.scalar.activation(vals_got[b][:], vals_raw[b][:].indirect(key_list[:]), COPY)
        vals_bf = []
        for pair in range(2):
            turned = bank(pair, [P, 2, 2, P], "turned%d" % pair)
            for b in range(2):
                words = vals_got[2 * pair + b][:].bitcast(F32)
                for u in range(2):
                    nc.tensor.transpose(turned[:, b, u, :], words[:, u : I // 2 : 2], ident[:])
            vals_bf.append(tile([P, 2, P, 2], F32, "vals_bf%d" % pair, AT_VALS3 + 2048 * pair))
            nc.scalar.copy(vals_bf[pair][:], turned[:].rearrange("p b u e -> p b e u"))

        table_q = weave_and_quantise(table_planes, "table")
        vals_q = []
        for pair in range(2):
            codes, scales = quantise(
                vals_bf[pair][:].rearrange("p b e u -> p (b e u)").bitcast(BF16),
                2 * P,
                "vals%d" % pair,
            )
            for b in range(2):
                vals_q.append((codes[:, P * b : P * (b + 1)], scales[:, P * b : P * (b + 1)]))

        for b in range(E // P):
            acc = bank(PACK + b, [P, J], "out_acc%d" % b)
            for h, cols in enumerate(HALVES):
                nc.tensor.matmul_mx(
                    out=acc[:, cols],
                    lhsT=vals_q[b][0].bitcast(FP8X4),
                    lhsT_scale=vals_q[b][1],
                    rhs=table_q[h][0][:].bitcast(FP8X4),
                    rhs_scale=table_q[h][1][:],
                    start=True,
                    stop=True,
                )
            result = tile([P, J], F32, "result%d" % b)
            if b % 2 == 0:
                nc.scalar.copy(result[:], acc[:])
            else:
                nc.vector.tensor_copy(result[:], acc[:])
            nc.sync.dma_start(out=out[P * b : P * (b + 1), :], in_=result[:])
